import numpy as np
import ml_dtypes


def mxq(x, axis, fmt="e4m3"):
    dtype, down = {"e4m3": (ml_dtypes.float8_e4m3fn, 7), "e5m2": (ml_dtypes.float8_e5m2, 14)}[fmt]
    v = np.moveaxis(np.asarray(x, np.float32).astype(ml_dtypes.bfloat16).astype(np.float64), axis, -1)
    blocks = v.reshape(v.shape[:-1] + (-1, 32))
    amax = np.abs(blocks).max(-1, keepdims=True)
    byte = np.maximum(np.where(amax > 0, np.frexp(amax)[1] - 1 + 127, 0) - down, 1)
    scale = np.exp2(byte - 127.0)
    codes = (blocks / scale).astype(np.float32).astype(dtype).astype(np.float64)
    return np.moveaxis((codes * scale).reshape(v.shape), -1, axis)


WIDE = False


def mx_kscale(k):
    if not WIDE:
        return np.ones(k)
    levels = np.array([10, -10, 5, -5, 0])
    if k % 512:
        return np.exp2(np.random.permutation(np.resize(levels, k // 32))).repeat(32)
    a = np.empty((k // 512, 16))
    for p in range(k // 512):
        a[p, :8] = np.random.permutation(np.resize(levels, 8))
        for g in range(8):
            far = levels[np.abs(levels - a[p, g]) >= 10]
            a[p, g + 8] = far[np.random.randint(len(far))]
    return np.exp2(a.ravel()).repeat(32)


def f64(x):
    return np.asarray(x).astype(np.float64)


def striped(idx):
    return np.tile(idx.reshape(-1, 16).T, (8, 1)).astype(np.uint16)


def unstriped(offs):
    return offs[:16].T.reshape(-1).astype(np.int64)


def striped8(idx):
    return np.concatenate([x.reshape(-1, 16).T for x in idx]).astype(np.uint16)


def runs(offs, k):
    lists = np.stack([offs[16 * r : 16 * r + 16].T.reshape(-1) for r in range(8)]).astype(np.int64)
    return lists[np.arange(k) % 512 // 64]


def pack_weight(w):
    k, n = w.shape
    w = f64(np.asarray(w, np.float32).astype(ml_dtypes.bfloat16)).reshape(k // 32, 32, n)
    amax = np.abs(w).max(1)
    byte = np.clip(np.where(amax > 0, np.frexp(amax)[1] - 1 + 127 - 7, 1), 1, 254)
    scaled = (w * np.exp2(127.0 - byte)[:, None, :]).reshape(k, n).astype(np.float32)
    words = np.ascontiguousarray(scaled.reshape(k // 512, 128, 4, n).transpose(0, 1, 3, 2)).astype(ml_dtypes.float8_e4m3fn).view(np.uint8)
    return words, np.ascontiguousarray(byte.astype(np.uint8).reshape(k // 512, 16, n))


def unpack_weight(words, scales):
    g, p, n, _ = words.shape
    vals = np.ascontiguousarray(words).view(ml_dtypes.float8_e4m3fn).astype(np.float64) * np.repeat(np.exp2(scales.astype(np.float64) - 127.0), 8, axis=1)[..., None]
    return vals.transpose(0, 1, 3, 2).reshape(g * 512, n)


E2M1 = np.array([0.0, 0.5, 1.0, 1.5, 2.0, 3.0, 4.0, 6.0, -0.0, -0.5, -1.0, -1.5, -2.0, -3.0, -4.0, -6.0])


def pack_fp4(w):
    k, n = w.shape
    w = f64(np.asarray(w, np.float32).astype(ml_dtypes.bfloat16)).reshape(k // 32, 32, n)
    amax = np.abs(w).max(1)
    mant, ex = np.frexp(amax / 6.0)
    byte = np.clip(np.where(amax > 0, np.where(mant > 0.5, ex, ex - 1) + 127, 1), 1, 254)
    scaled = (w * np.exp2(127.0 - byte)[:, None, :]).reshape(k, n).astype(np.float32)
    c = np.ascontiguousarray(scaled.reshape(k // 512, 128, 4, n).transpose(0, 1, 3, 2)).astype(ml_dtypes.float4_e2m1fn).view(np.uint8) & 0xF
    words = (c[..., 0::2] | (c[..., 1::2] << 4)).reshape(k // 512, 128, 2 * n)
    return np.ascontiguousarray(words), np.ascontiguousarray(byte.astype(np.uint8).reshape(k // 512, 16, n))


def unpack_fp4(words, scales):
    g, _, n = scales.shape
    words = np.ascontiguousarray(words).reshape(g, 128, n, 2)
    nib = np.empty((g, 128, n, 4), np.uint8)
    nib[..., 0::2] = words & 0xF
    nib[..., 1::2] = words >> 4
    vals = E2M1[nib] * np.repeat(np.exp2(scales.astype(np.float64) - 127.0), 8, axis=1)[..., None]
    return vals.transpose(0, 1, 3, 2).reshape(g * 512, n)


def silu(v):
    return v / (1.0 + np.exp(-np.maximum(v, -700.0)))

def planes(y):
    n, m = y.shape
    v = y.astype(np.float32).astype(ml_dtypes.bfloat16).astype(np.float64).reshape(n // 32, 32, m)
    top = np.abs(v).max(1)
    byte = np.clip(np.where(top > 0, np.frexp(top)[1] - 1 + 127 - 7, 1), 1, 254)
    codes = (v * np.exp2(127.0 - byte)[:, None, :]).reshape(n, m).astype(np.float32).astype(ml_dtypes.float8_e4m3fn).view(np.uint8)
    words = codes.reshape(n // 512, 128, 4, m).transpose(0, 1, 3, 2)
    return np.ascontiguousarray(words), np.ascontiguousarray(byte.astype(np.uint8).reshape(n // 512, 16, m))


K, T, S, V, H = 512, 2048, 512, 512, 512


def setup_inputs():
    n = np.random.standard_normal
    s = mx_kscale(K)[:, None]
    u = mx_kscale(H)
    packed_xT = pack_weight(n((K, T)) * s)
    packed_w2 = pack_fp4(n((H, H)) / np.sqrt(H) / u[:, None])
    return {
        "x_words": packed_xT[0],
        "x_scales": packed_xT[1],
        "w1": (n((K, H)) / np.sqrt(K) / s * u).astype(np.float32),
        "w2_words": packed_w2[0],
        "w2_scales": packed_w2[1],
        "gs": (np.random.uniform(0.5, 1.5, (K, 1)) / s).astype(np.float32),
        "pri": n((V, S)).astype(np.float32),
        "offs": striped(np.random.permutation(T)[:S]),
        "nb": striped8(np.stack([np.random.permutation(S) for _ in range(8)])),
        "cand": striped(np.random.permutation(T)[:V]),
    }


def reference(x_words, x_scales, w1, w2_words, w2_scales, gs, pri, offs, nb, cand):
    x_cand = unpack_weight(x_words, x_scales)[:, unstriped(cand)]
    xq = unpack_weight(x_words, x_scales)[:, unstriped(offs)]
    h = mxq(f64(w1), 0, "e4m3").T @ xq
    z = h[np.arange(H)[:, None], runs(nb, H)]
    h2 = silu(unpack_fp4(w2_words, w2_scales).T @ mxq(z, 0, "e4m3"))
    z2 = f64(gs) * h2
    out_0 = f64(pri) + 0.0625 * ((x_cand.T @ mxq(z2, 0, "e4m3")))
    return (out_0,) + planes(out_0)

@@ -1,0 +1,210 @@
+from contextlib import ExitStack
+
+import concourse.mybir as mybir
+
+F32 = mybir.dt.float32
+BF16 = mybir.dt.bfloat16
+I32 = mybir.dt.int32
+U32 = mybir.dt.uint32
+U16 = mybir.dt.uint16
+U8 = mybir.dt.uint8
+FP8X4 = mybir.dt.float8_e4m3fn_x4
+FP4X4 = mybir.dt.float4_e2m1fn_x4
+ACT = mybir.ActivationFunctionType
+ALU = mybir.AluOpType
+
+K, T, S, V, H = 512, 2048, 512, 512, 512
+FLOPS = 2 * K * H * S + 2 * H * H * S + 2 * K * V * S
+
+P = 128
+PACK = 4
+CHUNK = 128
+CHUNKS = S // CHUNK
+HALF = 256
+LIST_ROWS = 16
+
+
+def tile_picked_candnbr_silu_po_kernel(
+    tc, x_words, x_scales, w1, w2_words, w2_scales, gs, pri, offs, nb, cand, out_0, out_1, out_2
+):
+    nc = tc.nc
+    with ExitStack() as ctx:
+        keep = ctx.enter_context(tc.tile_pool(name="keep", bufs=1))
+        psum = ctx.enter_context(tc.psum_pool(name="psum", bufs=1))
+
+        def sb(name, shape, dtype, tag=None):
+            return keep.tile(shape, dtype, name=name, tag=tag or name, align_bytes=64)
+
+        def load_scale_rows(queue, plane, rows):
+            for q in range(4):
+                queue.dma_start(out=plane[32 * q : 32 * q + 4, :].bitcast(I32), in_=rows[4 * q : 4 * q + 4, :].bitcast(I32))
+
+        xs = sb("xs", [P, T], U8)
+        nc.gpsimd.memset(xs[:, : T // 2].bitcast(I32), 0)
+        nc.vector.memset(xs[:, T // 2 :].bitcast(I32), 0)
+        w2s_raw = sb("w2s_raw", [P, H], U8)
+        nc.gpsimd.memset(w2s_raw[:].bitcast(I32), 0)
+        warm_in = sb("warm_in", [P, 1], F32)
+        warm_out = sb("warm_out", [P, 1], F32)
+        nc.vector.memset(warm_in[:], 0.0)
+        nc.scalar.activation(out=warm_out[:], in_=warm_in[:], func=ACT.Silu)
+        offs_t = sb("offs_t", [P, S // 16], U16)
+        cand_t = sb("cand_t", [P, V // 16], U16)
+        nb_t = sb("nb_t", [P, S // 16], U16)
+        nc.sync.dma_start(offs_t[:], offs)
+        nc.sync.dma_start(cand_t[:], cand)
+        w1_rows = w1.rearrange("(p j) c -> p j c", j=PACK)
+        w1_raw = [sb(f"w1_raw{a}", [P, PACK, HALF], F32, tag=f"big{a}") for a in range(2)]
+        nc.sync.dma_start(out=w1_raw[0][:], in_=w1_rows[:, :, :HALF])
+        load_scale_rows(nc.sync, xs, x_scales[0])
+        nc.sync.dma_start(out=w1_raw[1][:], in_=w1_rows[:, :, HALF:])
+        xw = sb("xw", [P, T], U32)
+        nc.sync.dma_start(out=xw[:].bitcast(I32), in_=x_words[0].rearrange("p n t -> p (n t)").bitcast(I32))
+        nc.sync.dma_start(nb_t[:], nb)
+        w2w_raw = sb("w2w_raw", [P, 2 * H], U8)
+        nc.sync.dma_start(out=w2w_raw[:].bitcast(I32), in_=w2_words[0].bitcast(I32))
+        load_scale_rows(nc.sync, w2s_raw, w2_scales[0])
+        gs_t = sb("gs_t", [P, PACK], F32)
+        nc.sync.dma_start(out=gs_t[:], in_=gs.rearrange("(p t) o -> p (t o)", t=PACK))
+
+        xq_s = sb("xq_s", [P, S], U8)
+        xc_s = sb("xc_s", [P, V], U8)
+        nc.vector.tensor_copy(xq_s[:], xs[:].indirect(offs_t[:]))
+        nc.vector.tensor_copy(xc_s[:].rearrange("p (t m) -> p m t", t=PACK), xs[:].indirect(cand_t[:]))
+
+        w1g = sb("w1g", [P, PACK, P, PACK], BF16)
+        for a in range(2):
+            nc.scalar.copy(
+                out=w1g[:, :, 64 * a : 64 * (a + 1), :].rearrange("p t m j -> p m j t"),
+                in_=w1_raw[a][:].rearrange("p j (m t) -> p m j t", t=PACK),
+            )
+        w1q = sb("w1q", [P, H], U32)
+        w1s = sb("w1s", [P, H], U8)
+        nc.vector.quantize_mx(out=w1q[:].bitcast(FP8X4), scales=w1s[:], in_=w1g[:].rearrange("p t m j -> p (t m j)"))
+
+        w2w = sb("w2w", [P, 2 * H], U8)
+        nc.scalar.copy(
+            out=w2w[:].bitcast(U16).rearrange("p (t m) -> p m t", t=PACK),
+            in_=w2w_raw[:].bitcast(U16).rearrange("p (m t) -> p m t", t=PACK),
+        )
+
+        xq_w = [sb(f"xq_w{a}", [P, HALF], U32) for a in range(2)]
+        for a in range(2):
+            nc.vector.tensor_copy(xq_w[a][:], xw[:].indirect(offs_t[:, a * HALF // LIST_ROWS : (a + 1) * HALF // LIST_ROWS]))
+        xc_w = sb("xc_w", [P, V], U32)
+        nc.vector.tensor_copy(xc_w[:].rearrange("p (t m) -> p m t", t=PACK), xw[:].indirect(cand_t[:]))
+
+        w2s = sb("w2s", [P, H], U8)
+        nc.vector.tensor_copy(
+            out=w2s[:].rearrange("p (t m) -> p t m", t=PACK), in_=w2s_raw[:].rearrange("p (m t) -> p t m", t=PACK)
+        )
+
+        pri_rows = pri.rearrange("(p t) j -> p t j", t=PACK)
+        pri_t = []
+        for a in range(2):
+            half = sb(f"pri{a}", [P, PACK, HALF], F32, tag=f"big{a}")
+            nc.sync.dma_start(out=half[:], in_=pri_rows[:, :, a * HALF : (a + 1) * HALF])
+            pri_t.append(half)
+
+        h = [sb(f"h{t}", [P, S], F32) for t in range(PACK)]
+
+        def first(t, a):
+            cols = slice(t * P, (t + 1) * P)
+            places = slice(a * HALF, (a + 1) * HALF)
+            bank = psum.tile([P, HALF], F32, name=f"h_bank{t}{a}", tag=f"bank{2 * t + a}")
+            nc.tensor.matmul_mx(
+                out=bank[:], lhsT=w1q[:, cols].bitcast(FP8X4), lhsT_scale=w1s[:, cols],
+                rhs=xq_w[a][:].bitcast(FP8X4), rhs_scale=xq_s[:, places], start=True, stop=True,
+            )
+            nc.scalar.copy(out=h[t][:, places], in_=bank[:])
+
+        for t, a in [(0, 0), (1, 0), (0, 1), (1, 1), (2, 0), (2, 1), (3, 0), (3, 1)]:
+            first(t, a)
+
+        z_planes = [sb(f"z_planes{c}", [P, PACK, CHUNK], BF16) for c in range(CHUNKS)]
+        z_in = [sb(f"z_in{c}", [P, CHUNK, PACK], BF16) for c in range(CHUNKS)]
+        z_q = [sb(f"z_q{c}", [P, CHUNK], U32) for c in range(CHUNKS)]
+        z_s = [sb(f"z_s{c}", [P, CHUNK], U8) for c in range(CHUNKS)]
+        act = [sb(f"act{c}", [P, CHUNK, PACK], F32) for c in range(CHUNKS)]
+        z2_in = [sb(f"z2_in{c}", [P, CHUNK, PACK], BF16) for c in range(CHUNKS)]
+        z2_q = [sb(f"z2_q{c}", [P, CHUNK], U32) for c in range(CHUNKS)]
+        z2_s = [sb(f"z2_s{c}", [P, CHUNK], U8) for c in range(CHUNKS)]
+        res = [sb(f"res{c}", [P, PACK, CHUNK], F32) for c in range(CHUNKS)]
+        res_in = [sb(f"res_in{c}", [P, CHUNK, PACK], BF16) for c in range(CHUNKS)]
+        res_q = sb("res_q", [P, S], U32)
+        res_s = sb("res_s", [P, S], U8)
+        u_bank = {}
+        s_bank = {}
+        out_rows = out_0.rearrange("(p t) j -> p t j", t=PACK)
+        out_words = out_1[0].rearrange("p n t -> p (n t)").bitcast(I32)
+
+        def interleave(engine_copy, dst, src):
+            engine_copy(out=dst[:].rearrange("p (c i) t -> p c t i", i=4), in_=src[:].rearrange("p t (c i) -> p c t i", i=4))
+
+        def quantise(codes, scales, src):
+            nc.vector.quantize_mx(out=codes.bitcast(FP8X4), scales=scales, in_=src[:].rearrange("p n t -> p (n t)"))
+
+        def fetch(c):
+            part = nb_t[:, c * CHUNK // LIST_ROWS : (c + 1) * CHUNK // LIST_ROWS]
+            for t in range(PACK):
+                if t < 2:
+                    nc.vector.tensor_copy(z_planes[c][:, t, :], h[t][:].indirect(part))
+                else:
+                    nc.scalar.activation(z_planes[c][:, t, :], h[t][:].indirect(part), ACT.Copy)
+
+        def weave_z(c):
+            interleave(nc.vector.tensor_copy, z_in[c], z_planes[c])
+
+        def second(c):
+            quantise(z_q[c][:], z_s[c][:], z_in[c])
+            u_bank[c] = psum.tile([P, PACK, CHUNK], F32, name=f"u_bank{c}", tag=f"bank{c}")
+            for t in range(PACK):
+                nc.tensor.matmul_mx(
+                    out=u_bank[c][:, t, :], lhsT=w2w[:, 2 * t * P : 2 * (t + 1) * P].bitcast(FP4X4),
+                    lhsT_scale=w2s[:, t * P : (t + 1) * P], rhs=z_q[c][:].bitcast(FP8X4), rhs_scale=z_s[c][:],
+                    start=True, stop=True,
+                )
+
+        def silu(c):
+            nc.scalar.activation(out=act[c][:], in_=u_bank[c][:].rearrange("p t n -> p n t"), func=ACT.Silu)
+
+        def weigh(c):
+            nc.vector.tensor_tensor(
+                out=z2_in[c][:], in0=act[c][:], in1=gs_t[:].unsqueeze(1).to_broadcast([P, CHUNK, PACK]), op=ALU.mult
+            )
+
+        def third(c):
+            quantise(z2_q[c][:], z2_s[c][:], z2_in[c])
+            s_bank[c] = psum.tile([P, PACK, CHUNK], F32, name=f"s_bank{c}", tag=f"bank{4 + c}")
+            for t in range(PACK):
+                cols = slice(t * P, (t + 1) * P)
+                nc.tensor.matmul_mx(
+                    out=s_bank[c][:, t, :], lhsT=xc_w[:, cols].bitcast(FP8X4), lhsT_scale=xc_s[:, cols],
+                    rhs=z2_q[c][:].bitcast(FP8X4), rhs_scale=z2_s[c][:], start=True, stop=True,
+                )
+
+        def score(c):
+            a, lo = divmod(c * CHUNK, HALF)
+            nc.vector.scalar_tensor_tensor(
+                out=res[c][:], in0=s_bank[c][:], scalar=0.0625, in1=pri_t[a][:, :, lo : lo + CHUNK], op0=ALU.mult, op1=ALU.add
+            )
+            nc.sync.dma_start(out=out_rows[:, :, c * CHUNK : (c + 1) * CHUNK], in_=res[c][:])
+
+        def weave_out(c):
+            interleave(nc.scalar.copy, res_in[c], res[c])
+
+        def planes(c):
+            cols = slice(c * CHUNK, (c + 1) * CHUNK)
+            quantise(res_q[:, cols], res_s[:, cols], res_in[c])
+            nc.sync.dma_start(out=out_words[:, cols], in_=res_q[:, cols].bitcast(I32))
+
+        stages = [fetch, weave_z, second, silu, weigh, third, score, weave_out, planes]
+        for step in range(CHUNKS + len(stages) - 1):
+            for depth in reversed(range(len(stages))):
+                c = step - depth
+                if 0 <= c < CHUNKS:
+                    stages[depth](c)
+
+        for q in range(4):
+            queue = nc.scalar if q % 2 else nc.sync
+            queue.dma_start(out=out_2[0, 4 * q : 4 * q + 4, :].bitcast(I32), in_=res_s[32 * q : 32 * q + 4, :].bitcast(I32))

@@ -130,7 +130,7 @@ def tile_picked_candnbr_silu_po_kernel(
         z2_q = [sb(f"z2_q{c}", [P, CHUNK], U32) for c in range(CHUNKS)]
         z2_s = [sb(f"z2_s{c}", [P, CHUNK], U8) for c in range(CHUNKS)]
         res = [sb(f"res{c}", [P, PACK, CHUNK], F32) for c in range(CHUNKS)]
-        res_in = [sb(f"res_in{c}", [P, CHUNK, PACK], BF16) for c in range(CHUNKS)]
+        res_in = sb("res_in", [P, S, PACK], BF16)
         res_q = sb("res_q", [P, S], U32)
         res_s = sb("res_s", [P, S], U8)
         u_bank = {}
@@ -139,24 +139,24 @@ def tile_picked_candnbr_silu_po_kernel(
         out_words = out_1[0].rearrange("p n t -> p (n t)").bitcast(I32)
 
         def interleave(engine_copy, dst, src):
-            engine_copy(out=dst[:].rearrange("p (c i) t -> p c t i", i=4), in_=src[:].rearrange("p t (c i) -> p c t i", i=4))
+            engine_copy(out=dst.rearrange("p (c i) t -> p c t i", i=4), in_=src.rearrange("p t (c i) -> p c t i", i=4))
 
         def quantise(codes, scales, src):
-            nc.vector.quantize_mx(out=codes.bitcast(FP8X4), scales=scales, in_=src[:].rearrange("p n t -> p (n t)"))
+            nc.vector.quantize_mx(out=codes.bitcast(FP8X4), scales=scales, in_=src.rearrange("p n t -> p (n t)"))
 
         def fetch(c):
             part = nb_t[:, c * CHUNK // LIST_ROWS : (c + 1) * CHUNK // LIST_ROWS]
             for t in range(PACK):
-                if t < 2:
+                if t < (2 if c < 3 else 1):
                     nc.vector.tensor_copy(z_planes[c][:, t, :], h[t][:].indirect(part))
                 else:
                     nc.scalar.activation(z_planes[c][:, t, :], h[t][:].indirect(part), ACT.Copy)
 
         def weave_z(c):
-            interleave(nc.vector.tensor_copy, z_in[c], z_planes[c])
+            interleave(nc.vector.tensor_copy, z_in[c][:], z_planes[c][:])
 
         def second(c):
-            quantise(z_q[c][:], z_s[c][:], z_in[c])
+            quantise(z_q[c][:], z_s[c][:], z_in[c][:])
             u_bank[c] = psum.tile([P, PACK, CHUNK], F32, name=f"u_bank{c}", tag=f"bank{c}")
             for t in range(PACK):
                 nc.tensor.matmul_mx(
@@ -174,7 +174,7 @@ def tile_picked_candnbr_silu_po_kernel(
             )
 
         def third(c):
-            quantise(z2_q[c][:], z2_s[c][:], z2_in[c])
+            quantise(z2_q[c][:], z2_s[c][:], z2_in[c][:])
             s_bank[c] = psum.tile([P, PACK, CHUNK], F32, name=f"s_bank{c}", tag=f"bank{4 + c}")
             for t in range(PACK):
                 cols = slice(t * P, (t + 1) * P)
@@ -191,20 +191,19 @@ def tile_picked_candnbr_silu_po_kernel(
             nc.sync.dma_start(out=out_rows[:, :, c * CHUNK : (c + 1) * CHUNK], in_=res[c][:])
 
         def weave_out(c):
-            interleave(nc.scalar.copy, res_in[c], res[c])
+            interleave(nc.scalar.copy, res_in[:, c * CHUNK : (c + 1) * CHUNK, :], res[c][:])
 
-        def planes(c):
-            cols = slice(c * CHUNK, (c + 1) * CHUNK)
-            quantise(res_q[:, cols], res_s[:, cols], res_in[c])
+        def planes(cols):
+            quantise(res_q[:, cols], res_s[:, cols], res_in[:, cols, :])
             nc.sync.dma_start(out=out_words[:, cols], in_=res_q[:, cols].bitcast(I32))
 
-        stages = [fetch, weave_z, second, silu, weigh, third, score, weave_out, planes]
-        for step in range(CHUNKS + len(stages) - 1):
-            for depth in reversed(range(len(stages))):
-                c = step - depth
-                if 0 <= c < CHUNKS:
-                    stages[depth](c)
+        for group in ([fetch, weave_z, second], [silu], [weigh, third], [score, weave_out]):
+            for c in range(CHUNKS):
+                for stage in group:
+                    stage(c)
+        planes(slice(0, S - CHUNK))
+        planes(slice(S - CHUNK, S))
 
         for q in range(4):
-            queue = nc.scalar if q % 2 else nc.sync
+            queue = nc.sync if q % 2 else nc.scalar
             queue.dma_start(out=out_2[0, 4 * q : 4 * q + 4, :].bitcast(I32), in_=res_s[32 * q : 32 * q + 4, :].bitcast(I32))

@@ -39,6 +39,17 @@ def tile_picked_candnbr_silu_po_kernel(
             for q in range(4):
                 queue.dma_start(out=plane[32 * q : 32 * q + 4, :].bitcast(I32), in_=rows[4 * q : 4 * q + 4, :].bitcast(I32))
 
+        def interleave(engine_copy, dst, src):
+            engine_copy(out=dst.rearrange("p (c i) t -> p c t i", i=4), in_=src.rearrange("p t (c i) -> p c t i", i=4))
+
+        def quantise(codes, scales, src):
+            nc.vector.quantize_mx(out=codes.bitcast(FP8X4), scales=scales, in_=src.rearrange("p n t -> p (n t)"))
+
+        def deal(engine_copy, dst, src, run):
+            engine_copy(
+                out=dst.rearrange("p (t g i) -> p g t i", t=PACK, i=run), in_=src.rearrange("p (g i t) -> p g t i", t=PACK, i=run)
+            )
+
         xs = sb("xs", [P, T], U8)
         nc.gpsimd.memset(xs[:, : T // 2].bitcast(I32), 0)
         nc.vector.memset(xs[:, T // 2 :].bitcast(I32), 0)
@@ -68,25 +79,24 @@ def tile_picked_candnbr_silu_po_kernel(
         nc.sync.dma_start(out=gs_t[:], in_=gs.rearrange("(p t) o -> p (t o)", t=PACK))
 
         xq_s = sb("xq_s", [P, S], U8)
-        xc_s = sb("xc_s", [P, V], U8)
         nc.vector.tensor_copy(xq_s[:], xs[:].indirect(offs_t[:]))
-        nc.vector.tensor_copy(xc_s[:].rearrange("p (t m) -> p m t", t=PACK), xs[:].indirect(cand_t[:]))
+        xc_s_listed = sb("xc_s_listed", [P, V], U8)
+        nc.vector.tensor_copy(xc_s_listed[:], xs[:].indirect(cand_t[:]))
 
-        w1g = sb("w1g", [P, PACK, P, PACK], BF16)
+        w1q_plain = sb("w1q_plain", [P, H], U32)
+        w1s_plain = sb("w1s_plain", [P, H], U8)
+        nc.gpsimd.memset(w1s_plain[:].bitcast(I32), 0)
+        w1_in = sb("w1_in", [P, H, PACK], BF16)
         for a in range(2):
-            nc.scalar.copy(
-                out=w1g[:, :, 64 * a : 64 * (a + 1), :].rearrange("p t m j -> p m j t"),
-                in_=w1_raw[a][:].rearrange("p j (m t) -> p m j t", t=PACK),
-            )
+            interleave(nc.scalar.copy, w1_in[:, a * HALF : (a + 1) * HALF, :], w1_raw[a][:])
+        quantise(w1q_plain[:], w1s_plain[:], w1_in[:])
         w1q = sb("w1q", [P, H], U32)
         w1s = sb("w1s", [P, H], U8)
-        nc.vector.quantize_mx(out=w1q[:].bitcast(FP8X4), scales=w1s[:], in_=w1g[:].rearrange("p t m j -> p (t m j)"))
+        deal(nc.vector.tensor_copy, w1s[:], w1s_plain[:], 16)
+        deal(nc.scalar.copy, w1q[:], w1q_plain[:], 4)
 
         w2w = sb("w2w", [P, 2 * H], U8)
-        nc.scalar.copy(
-            out=w2w[:].bitcast(U16).rearrange("p (t m) -> p m t", t=PACK),
-            in_=w2w_raw[:].bitcast(U16).rearrange("p (m t) -> p m t", t=PACK),
-        )
+        deal(nc.scalar.copy, w2w[:].bitcast(U16), w2w_raw[:].bitcast(U16), 8)
 
         xq_w = [sb(f"xq_w{a}", [P, HALF], U32) for a in range(2)]
         for a in range(2):
@@ -94,10 +104,10 @@ def tile_picked_candnbr_silu_po_kernel(
         xc_w = sb("xc_w", [P, V], U32)
         nc.vector.tensor_copy(xc_w[:].rearrange("p (t m) -> p m t", t=PACK), xw[:].indirect(cand_t[:]))
 
+        xc_s = sb("xc_s", [P, V], U8, tag="xw")
+        deal(nc.vector.tensor_copy, xc_s[:], xc_s_listed[:], 16)
         w2s = sb("w2s", [P, H], U8)
-        nc.vector.tensor_copy(
-            out=w2s[:].rearrange("p (t m) -> p t m", t=PACK), in_=w2s_raw[:].rearrange("p (m t) -> p t m", t=PACK)
-        )
+        deal(nc.vector.tensor_copy, w2s[:], w2s_raw[:], 16)
 
         pri_rows = pri.rearrange("(p t) j -> p t j", t=PACK)
         pri_t = []
@@ -137,12 +147,6 @@ def tile_picked_candnbr_silu_po_kernel(
         s_bank = {}
         out_rows = out_0.rearrange("(p t) j -> p t j", t=PACK)
         out_words = out_1[0].rearrange("p n t -> p (n t)").bitcast(I32)
-
-        def interleave(engine_copy, dst, src):
-            engine_copy(out=dst.rearrange("p (c i) t -> p c t i", i=4), in_=src.rearrange("p t (c i) -> p c t i", i=4))
-
-        def quantise(codes, scales, src):
-            nc.vector.quantize_mx(out=codes.bitcast(FP8X4), scales=scales, in_=src.rearrange("p n t -> p (n t)"))
 
         def fetch(c):
             part = nb_t[:, c * CHUNK // LIST_ROWS : (c + 1) * CHUNK // LIST_ROWS]

@@ -139,7 +139,7 @@ def tile_picked_candnbr_silu_po_kernel(
         z2_in = [sb(f"z2_in{c}", [P, CHUNK, PACK], BF16) for c in range(CHUNKS)]
         z2_q = [sb(f"z2_q{c}", [P, CHUNK], U32) for c in range(CHUNKS)]
         z2_s = [sb(f"z2_s{c}", [P, CHUNK], U8) for c in range(CHUNKS)]
-        res = [sb(f"res{c}", [P, PACK, CHUNK], F32) for c in range(CHUNKS)]
+        res = [sb(f"res{a}", [P, PACK, HALF], F32) for a in range(2)]
         res_in = sb("res_in", [P, S, PACK], BF16)
         res_q = sb("res_q", [P, S], U32)
         res_s = sb("res_s", [P, S], U8)
@@ -178,35 +178,45 @@ def tile_picked_candnbr_silu_po_kernel(
             )
 
         def third(c):
+            a, lo = divmod(c * CHUNK, HALF)
             quantise(z2_q[c][:], z2_s[c][:], z2_in[c][:])
-            s_bank[c] = psum.tile([P, PACK, CHUNK], F32, name=f"s_bank{c}", tag=f"bank{4 + c}")
             for t in range(PACK):
+                u, e = divmod(t, 2)
+                if (a, u) not in s_bank:
+                    s_bank[a, u] = psum.tile([P, 2, HALF], F32, name=f"s_bank{a}{u}", tag=f"bank{4 + 2 * a + u}")
                 cols = slice(t * P, (t + 1) * P)
                 nc.tensor.matmul_mx(
-                    out=s_bank[c][:, t, :], lhsT=xc_w[:, cols].bitcast(FP8X4), lhsT_scale=xc_s[:, cols],
+                    out=s_bank[a, u][:, e, lo : lo + CHUNK], lhsT=xc_w[:, cols].bitcast(FP8X4), lhsT_scale=xc_s[:, cols],
                     rhs=z2_q[c][:].bitcast(FP8X4), rhs_scale=z2_s[c][:], start=True, stop=True,
                 )
 
-        def score(c):
-            a, lo = divmod(c * CHUNK, HALF)
+        def score(a, u):
+            pair = slice(2 * u, 2 * u + 2)
             nc.vector.scalar_tensor_tensor(
-                out=res[c][:], in0=s_bank[c][:], scalar=0.0625, in1=pri_t[a][:, :, lo : lo + CHUNK], op0=ALU.mult, op1=ALU.add
+                out=res[a][:, pair, :], in0=s_bank[a, u][:], scalar=0.0625, in1=pri_t[a][:, pair, :], op0=ALU.mult, op1=ALU.add
             )
-            nc.sync.dma_start(out=out_rows[:, :, c * CHUNK : (c + 1) * CHUNK], in_=res[c][:])
+            nc.sync.dma_start(out=out_rows[:, pair, a * HALF : (a + 1) * HALF], in_=res[a][:, pair, :])
 
-        def weave_out(c):
-            interleave(nc.scalar.copy, res_in[:, c * CHUNK : (c + 1) * CHUNK, :], res[c][:])
+        def weave_out(engine_copy, c):
+            a, lo = divmod(c * CHUNK, HALF)
+            interleave(engine_copy, res_in[:, c * CHUNK : (c + 1) * CHUNK, :], res[a][:, :, lo : lo + CHUNK])
 
         def planes(cols):
             quantise(res_q[:, cols], res_s[:, cols], res_in[:, cols, :])
             nc.sync.dma_start(out=out_words[:, cols], in_=res_q[:, cols].bitcast(I32))
 
-        for group in ([fetch, weave_z, second], [silu], [weigh, third], [score, weave_out]):
+        for group in ([fetch, weave_z, second], [silu], [weigh, third]):
             for c in range(CHUNKS):
                 for stage in group:
                     stage(c)
-        planes(slice(0, S - CHUNK))
-        planes(slice(S - CHUNK, S))
+        for a in range(2):
+            for u in range(2):
+                score(a, u)
+        for c in range(CHUNKS - 1):
+            weave_out(nc.scalar.copy, c)
+        planes(slice(0, HALF))
+        weave_out(nc.vector.tensor_copy, CHUNKS - 1)
+        planes(slice(HALF, S))
 
         for q in range(4):
             queue = nc.sync if q % 2 else nc.scalar

from contextlib import ExitStack

import concourse.mybir as mybir

F32 = mybir.dt.float32
BF16 = mybir.dt.bfloat16
I32 = mybir.dt.int32
U32 = mybir.dt.uint32
U16 = mybir.dt.uint16
U8 = mybir.dt.uint8
FP8X4 = mybir.dt.float8_e4m3fn_x4
FP4X4 = mybir.dt.float4_e2m1fn_x4
ACT = mybir.ActivationFunctionType
ALU = mybir.AluOpType

K, T, S, V, H = 512, 2048, 512, 512, 512
FLOPS = 2 * K * H * S + 2 * H * H * S + 2 * K * V * S

P = 128
PACK = 4
CHUNK = 128
CHUNKS = S // CHUNK
HALF = 256
LIST_ROWS = 16


def tile_picked_candnbr_silu_po_kernel(
    tc, x_words, x_scales, w1, w2_words, w2_scales, gs, pri, offs, nb, cand, out_0, out_1, out_2
):
    nc = tc.nc
    with ExitStack() as ctx:
        keep = ctx.enter_context(tc.tile_pool(name="keep", bufs=1))
        psum = ctx.enter_context(tc.psum_pool(name="psum", bufs=1))

        def sb(name, shape, dtype, tag=None):
            return keep.tile(shape, dtype, name=name, tag=tag or name, align_bytes=64)

        def load_scale_rows(queue, plane, rows):
            for q in range(4):
                queue.dma_start(out=plane[32 * q : 32 * q + 4, :].bitcast(I32), in_=rows[4 * q : 4 * q + 4, :].bitcast(I32))

        def interleave(engine_copy, dst, src):
            engine_copy(out=dst.rearrange("p (c i) t -> p c t i", i=4), in_=src.rearrange("p t (c i) -> p c t i", i=4))

        def quantise(codes, scales, src):
            nc.vector.quantize_mx(out=codes.bitcast(FP8X4), scales=scales, in_=src.rearrange("p n t -> p (n t)"))

        def deal(engine_copy, dst, src, run):
            engine_copy(
                out=dst.rearrange("p (t g i) -> p g t i", t=PACK, i=run), in_=src.rearrange("p (g i t) -> p g t i", t=PACK, i=run)
            )

        xs = sb("xs", [P, T], U8)
        nc.gpsimd.memset(xs[:, : T // 2].bitcast(I32), 0)
        nc.vector.memset(xs[:, T // 2 :].bitcast(I32), 0)
        w2s_raw = sb("w2s_raw", [P, H], U8)
        nc.gpsimd.memset(w2s_raw[:].bitcast(I32), 0)
        warm_in = sb("warm_in", [P, 1], F32)
        warm_out = sb("warm_out", [P, 1], F32)
        nc.vector.memset(warm_in[:], 0.0)
        nc.scalar.activation(out=warm_out[:], in_=warm_in[:], func=ACT.Silu)
        offs_t = sb("offs_t", [P, S // 16], U16)
        cand_t = sb("cand_t", [P, V // 16], U16)
        nb_t = sb("nb_t", [P, S // 16], U16)
        nc.sync.dma_start(offs_t[:], offs)
        nc.sync.dma_start(cand_t[:], cand)
        w1_rows = w1.rearrange("(p j) c -> p j c", j=PACK)
        w1_raw = [sb(f"w1_raw{a}", [P, PACK, HALF], F32, tag=f"big{a}") for a in range(2)]
        nc.sync.dma_start(out=w1_raw[0][:], in_=w1_rows[:, :, :HALF])
        load_scale_rows(nc.sync, xs, x_scales[0])
        nc.sync.dma_start(out=w1_raw[1][:], in_=w1_rows[:, :, HALF:])
        xw = sb("xw", [P, T], U32)
        nc.sync.dma_start(out=xw[:].bitcast(I32), in_=x_words[0].rearrange("p n t -> p (n t)").bitcast(I32))
        nc.sync.dma_start(nb_t[:], nb)
        w2w_raw = sb("w2w_raw", [P, 2 * H], U8)
        nc.sync.dma_start(out=w2w_raw[:].bitcast(I32), in_=w2_words[0].bitcast(I32))
        load_scale_rows(nc.sync, w2s_raw, w2_scales[0])
        gs_t = sb("gs_t", [P, PACK], F32)
        nc.sync.dma_start(out=gs_t[:], in_=gs.rearrange("(p t) o -> p (t o)", t=PACK))

        xq_s = sb("xq_s", [P, S], U8)
        nc.vector.tensor_copy(xq_s[:], xs[:].indirect(offs_t[:]))
        xc_s_listed = sb("xc_s_listed", [P, V], U8)
        nc.vector.tensor_copy(xc_s_listed[:], xs[:].indirect(cand_t[:]))

        w1q_plain = sb("w1q_plain", [P, H], U32)
        w1s_plain = sb("w1s_plain", [P, H], U8)
        nc.gpsimd.memset(w1s_plain[:].bitcast(I32), 0)
        w1_in = sb("w1_in", [P, H, PACK], BF16)
        for a in range(2):
            interleave(nc.scalar.copy, w1_in[:, a * HALF : (a + 1) * HALF, :], w1_raw[a][:])
        quantise(w1q_plain[:], w1s_plain[:], w1_in[:])
        w1q = sb("w1q", [P, H], U32)
        w1s = sb("w1s", [P, H], U8)
        deal(nc.vector.tensor_copy, w1s[:], w1s_plain[:], 16)
        deal(nc.scalar.copy, w1q[:], w1q_plain[:], 4)

        w2w = sb("w2w", [P, 2 * H], U8)
        deal(nc.scalar.copy, w2w[:].bitcast(U16), w2w_raw[:].bitcast(U16), 8)

        xq_w = [sb(f"xq_w{a}", [P, HALF], U32) for a in range(2)]
        for a in range(2):
            nc.vector.tensor_copy(xq_w[a][:], xw[:].indirect(offs_t[:, a * HALF // LIST_ROWS : (a + 1) * HALF // LIST_ROWS]))
        xc_w = sb("xc_w", [P, V], U32)
        nc.vector.tensor_copy(xc_w[:].rearrange("p (t m) -> p m t", t=PACK), xw[:].indirect(cand_t[:]))

        xc_s = sb("xc_s", [P, V], U8, tag="xw")
        deal(nc.vector.tensor_copy, xc_s[:], xc_s_listed[:], 16)
        w2s = sb("w2s", [P, H], U8)
        deal(nc.vector.tensor_copy, w2s[:], w2s_raw[:], 16)

        pri_rows = pri.rearrange("(p t) j -> p t j", t=PACK)
        pri_t = []
        for a in range(2):
            half = sb(f"pri{a}", [P, PACK, HALF], F32, tag=f"big{a}")
            nc.sync.dma_start(out=half[:], in_=pri_rows[:, :, a * HALF : (a + 1) * HALF])
            pri_t.append(half)

        h = [sb(f"h{t}", [P, S], F32) for t in range(PACK)]

        def first(t, a):
            cols = slice(t * P, (t + 1) * P)
            places = slice(a * HALF, (a + 1) * HALF)
            bank = psum.tile([P, HALF], F32, name=f"h_bank{t}{a}", tag=f"bank{2 * t + a}")
            nc.tensor.matmul_mx(
                out=bank[:], lhsT=w1q[:, cols].bitcast(FP8X4), lhsT_scale=w1s[:, cols],
                rhs=xq_w[a][:].bitcast(FP8X4), rhs_scale=xq_s[:, places], start=True, stop=True,
            )
            nc.scalar.copy(out=h[t][:, places], in_=bank[:])

        for t, a in [(0, 0), (1, 0), (0, 1), (1, 1), (2, 0), (2, 1), (3, 0), (3, 1)]:
            first(t, a)

        z_planes = [sb(f"z_planes{c}", [P, PACK, CHUNK], BF16) for c in range(CHUNKS)]
        z_in = [sb(f"z_in{c}", [P, CHUNK, PACK], BF16) for c in range(CHUNKS)]
        z_q = [sb(f"z_q{c}", [P, CHUNK], U32) for c in range(CHUNKS)]
        z_s = [sb(f"z_s{c}", [P, CHUNK], U8) for c in range(CHUNKS)]
        act = [sb(f"act{c}", [P, CHUNK, PACK], F32) for c in range(CHUNKS)]
        z2_in = [sb(f"z2_in{c}", [P, CHUNK, PACK], BF16) for c in range(CHUNKS)]
        z2_q = [sb(f"z2_q{c}", [P, CHUNK], U32) for c in range(CHUNKS)]
        z2_s = [sb(f"z2_s{c}", [P, CHUNK], U8) for c in range(CHUNKS)]
        res = [sb(f"res{a}", [P, PACK, HALF], F32) for a in range(2)]
        res_in = sb("res_in", [P, S, PACK], BF16)
        res_q = sb("res_q", [P, S], U32)
        res_s = sb("res_s", [P, S], U8)
        u_bank = {}
        s_bank = {}
        out_rows = out_0.rearrange("(p t) j -> p t j", t=PACK)
        out_words = out_1[0].rearrange("p n t -> p (n t)").bitcast(I32)

        def fetch(c):
            part = nb_t[:, c * CHUNK // LIST_ROWS : (c + 1) * CHUNK // LIST_ROWS]
            for t in range(PACK):
                if t < (2 if c < 3 else 1):
                    nc.vector.tensor_copy(z_planes[c][:, t, :], h[t][:].indirect(part))
                else:
                    nc.scalar.activation(z_planes[c][:, t, :], h[t][:].indirect(part), ACT.Copy)

        def weave_z(c):
            interleave(nc.vector.tensor_copy, z_in[c][:], z_planes[c][:])

        def second(c):
            quantise(z_q[c][:], z_s[c][:], z_in[c][:])
            u_bank[c] = psum.tile([P, PACK, CHUNK], F32, name=f"u_bank{c}", tag=f"bank{c}")
            for t in range(PACK):
                nc.tensor.matmul_mx(
                    out=u_bank[c][:, t, :], lhsT=w2w[:, 2 * t * P : 2 * (t + 1) * P].bitcast(FP4X4),
                    lhsT_scale=w2s[:, t * P : (t + 1) * P], rhs=z_q[c][:].bitcast(FP8X4), rhs_scale=z_s[c][:],
                    start=True, stop=True,
                )

        def silu(c):
            nc.scalar.activation(out=act[c][:], in_=u_bank[c][:].rearrange("p t n -> p n t"), func=ACT.Silu)

        def weigh(c):
            nc.vector.tensor_tensor(
                out=z2_in[c][:], in0=act[c][:], in1=gs_t[:].unsqueeze(1).to_broadcast([P, CHUNK, PACK]), op=ALU.mult
            )

        def third(c):
            a, lo = divmod(c * CHUNK, HALF)
            quantise(z2_q[c][:], z2_s[c][:], z2_in[c][:])
            for t in range(PACK):
                u, e = divmod(t, 2)
                if (a, u) not in s_bank:
                    s_bank[a, u] = psum.tile([P, 2, HALF], F32, name=f"s_bank{a}{u}", tag=f"bank{4 + 2 * a + u}")
                cols = slice(t * P, (t + 1) * P)
                nc.tensor.matmul_mx(
                    out=s_bank[a, u][:, e, lo : lo + CHUNK], lhsT=xc_w[:, cols].bitcast(FP8X4), lhsT_scale=xc_s[:, cols],
                    rhs=z2_q[c][:].bitcast(FP8X4), rhs_scale=z2_s[c][:], start=True, stop=True,
                )

        def score(a, u):
            pair = slice(2 * u, 2 * u + 2)
            nc.vector.scalar_tensor_tensor(
                out=res[a][:, pair, :], in0=s_bank[a, u][:], scalar=0.0625, in1=pri_t[a][:, pair, :], op0=ALU.mult, op1=ALU.add
            )
            nc.sync.dma_start(out=out_rows[:, pair, a * HALF : (a + 1) * HALF], in_=res[a][:, pair, :])

        def weave_out(engine_copy, c):
            a, lo = divmod(c * CHUNK, HALF)
            interleave(engine_copy, res_in[:, c * CHUNK : (c + 1) * CHUNK, :], res[a][:, :, lo : lo + CHUNK])

        def planes(cols):
            quantise(res_q[:, cols], res_s[:, cols], res_in[:, cols, :])
            nc.sync.dma_start(out=out_words[:, cols], in_=res_q[:, cols].bitcast(I32))

        for group in ([fetch, weave_z, second], [silu], [weigh, third]):
            for c in range(CHUNKS):
                for stage in group:
                    stage(c)
        for a in range(2):
            for u in range(2):
                score(a, u)
        for c in range(CHUNKS - 1):
            weave_out(nc.scalar.copy, c)
        planes(slice(0, HALF))
        weave_out(nc.vector.tensor_copy, CHUNKS - 1)
        planes(slice(HALF, S))

        for q in range(4):
            queue = nc.sync if q % 2 else nc.scalar
            queue.dma_start(out=out_2[0, 4 * q : 4 * q + 4, :].bitcast(I32), in_=res_s[32 * q : 32 * q + 4, :].bitcast(I32))
